import numpy as np
import ml_dtypes


def mxq(x, axis, fmt="e4m3"):
    dtype, down = {"e4m3": (ml_dtypes.float8_e4m3fn, 7), "e5m2": (ml_dtypes.float8_e5m2, 14)}[fmt]
    v = np.moveaxis(np.asarray(x, np.float32).astype(ml_dtypes.bfloat16).astype(np.float64), axis, -1)
    blocks = v.reshape(v.shape[:-1] + (-1, 32))
    amax = np.abs(blocks).max(-1, keepdims=True)
    byte = np.maximum(np.where(amax > 0, np.frexp(amax)[1] - 1 + 127, 0) - down, 1)
    scale = np.exp2(byte - 127.0)
    codes = (blocks / scale).astype(np.float32).astype(dtype).astype(np.float64)
    return np.moveaxis((codes * scale).reshape(v.shape), -1, axis)


WIDE = False


def mx_kscale(k):
    if not WIDE:
        return np.ones(k)
    levels = np.array([30, -30])
    if k % 512:
        return np.exp2(np.random.permutation(np.resize(levels, k // 32))).repeat(32)
    a = np.empty((k // 512, 16))
    for p in range(k // 512):
        a[p, :8] = np.random.permutation(np.resize(levels, 8))
        for g in range(8):
            far = levels[np.abs(levels - a[p, g]) >= 10]
            a[p, g + 8] = far[np.random.randint(len(far))]
    return np.exp2(a.ravel()).repeat(32)


def f64(x):
    return np.asarray(x).astype(np.float64)


def striped(idx):
    return np.tile(np.asarray(idx).reshape(-1, 16).T, (8, 1)).astype(np.uint16)


def unstriped(offs):
    return offs[:16].T.reshape(-1).astype(np.int64)


E2M1 = np.array([0.0, 0.5, 1.0, 1.5, 2.0, 3.0, 4.0, 6.0, -0.0, -0.5, -1.0, -1.5, -2.0, -3.0, -4.0, -6.0])


def pack_weight(w, fmt):
    k, n = w.shape
    w = f64(np.asarray(w, np.float32).astype(ml_dtypes.bfloat16)).reshape(k // 32, 32, n)
    amax = np.abs(w).max(1)
    if fmt == "e4m3":
        byte = np.frexp(amax)[1] - 1 + 127 - 7
    else:
        mant, ex = np.frexp(amax / 6.0)
        byte = np.where(mant > 0.5, ex, ex - 1) + 127
    byte = np.clip(np.where(amax > 0, byte, 1), 1, 254)
    scaled = (w * np.exp2(127.0 - byte)[:, None, :]).reshape(k, n).astype(np.float32)
    by_word = np.ascontiguousarray(scaled.reshape(k // 512, 128, 4, n).transpose(0, 1, 3, 2))
    if fmt == "e4m3":
        words = by_word.astype(ml_dtypes.float8_e4m3fn).view(np.uint8)
    else:
        c = by_word.astype(ml_dtypes.float4_e2m1fn).view(np.uint8) & 0xF
        words = (c[..., 0::2] | (c[..., 1::2] << 4)).reshape(k // 512, 128, 2 * n)
    return np.ascontiguousarray(words), np.ascontiguousarray(byte.astype(np.uint8).reshape(k // 512, 16, n))


def unpack_weight(words, scales, fmt):
    g, _, n = scales.shape
    words = np.ascontiguousarray(words).reshape(g, 128, n, -1)
    if fmt == "e4m3":
        vals = words.view(ml_dtypes.float8_e4m3fn).astype(np.float64)
    else:
        nib = np.empty((g, 128, n, 4), np.uint8)
        nib[..., 0::2] = words & 0xF
        nib[..., 1::2] = words >> 4
        vals = E2M1[nib]
    vals = vals * np.repeat(np.exp2(scales.astype(np.float64) - 127.0), 8, axis=1)[..., None]
    return vals.transpose(0, 1, 3, 2).reshape(g * 512, n)


K, R, N, T, J = 1024, 128, 1024, 2048, 512


def setup_inputs():
    n = np.random.standard_normal
    idx = np.random.permutation(T)[:J]
    fk = mx_kscale(K)
    fj = mx_kscale(J)
    tj = np.ones(T)
    tj[idx] = fj
    xtp = pack_weight(n((K, T)) / fk[:, None], "e2m1")
    lowp = pack_weight(n((K, R)) * 1 / np.sqrt(K) * fk[:, None], "e4m3")
    return {
        "xt_words": xtp[0],
        "xt_scales": xtp[1],
        "low_words": lowp[0],
        "low_scales": lowp[1],
        "cj": (np.random.uniform(0.5, 2.0, (1, J)) * fj).astype(np.float32),
        "g": (n((N, T)) * np.exp(0.5 * n((1, T))) / tj).astype(np.float32),
        "old": (1.0 * n((R, N))).astype(np.float32),
        "offs": striped(idx),
    }


def reference(xt_words, xt_scales, low_words, low_scales, cj, g, old, offs):
    idx = unstriped(offs)
    xtu = unpack_weight(xt_words, xt_scales, "e2m1")
    lowu = unpack_weight(low_words, low_scales, "e4m3")
    xtidxg = xtu[:, idx]
    u = lowu.T @ xtidxg
    uw = u * f64(cj)
    ut = uw.T
    gj = f64(g)[:, idx].T
    utq = mxq(ut, 0, "e4m3")
    gjq = mxq(gj, 0, "e5m2")
    w = utq.T @ gjq
    y = 0.04 * w + 0.5 * f64(old)
    return y

@@ -1,0 +1,179 @@
+from contextlib import ExitStack
+
+import concourse.mybir as mybir
+from concourse.masks import make_identity
+
+K, R, N, T, J = 1024, 128, 1024, 2048, 512
+FLOPS = 2 * K * R * J + 2 * J * R * N
+
+F32 = mybir.dt.float32
+BF16 = mybir.dt.bfloat16
+I32 = mybir.dt.int32
+U32 = mybir.dt.uint32
+U16 = mybir.dt.uint16
+U8 = mybir.dt.uint8
+E4M3 = mybir.dt.float8_e4m3fn_x4
+E5M2 = mybir.dt.float8_e5m2_x4
+E2M1 = mybir.dt.float4_e2m1fn_x4
+MULT = mybir.AluOpType.mult
+ADD = mybir.AluOpType.add
+COPY = mybir.ActivationFunctionType.Copy
+
+P = 128
+PACK = 4
+PASSES = K // (P * PACK)
+G_TILES = N // P
+MOVING = 512
+W_SHARE = 0.04
+OLD_SHARE = 0.5
+U_AFTER = 3
+
+
+def tile_list_adapter_up_grad_kernel(tc, xt_words, xt_scales, low_words, low_scales, cj, g, old, offs, out):
+    nc = tc.nc
+    with ExitStack() as ctx:
+        keep = ctx.enter_context(tc.tile_pool(name="keep", bufs=1))
+        ring = ctx.enter_context(tc.tile_pool(name="ring", bufs=3))
+        psum = ctx.enter_context(tc.psum_pool(name="psum", bufs=1))
+
+        offsets = keep.tile([P, J // 16], U16, name="offsets")
+        x_words = [keep.tile([P, T], U16, name="x_words%d" % z, align_bytes=64) for z in range(PASSES)]
+        x_rows = keep.tile([P, T], U8, name="x_rows", align_bytes=64)
+        low_codes = keep.tile([P, PASSES, R], U32, name="low_codes", align_bytes=64)
+        low_plane = keep.tile([P, PASSES, R], U8, name="low_plane", align_bytes=64)
+        x_plane = keep.tile([P, PASSES, J], U8, name="x_plane", align_bytes=64)
+        weights = keep.tile([P, PACK], F32, name="weights")
+        g_rows = [keep.tile([P, T], F32, name="g_rows%d" % i, align_bytes=64) for i in range(G_TILES)]
+        ident = keep.tile([P, P], F32, name="ident")
+
+        last = slice(N - P, N)
+        parts = [(0, slice(0, MOVING)), (N - P - MOVING, slice(MOVING, N - P)), (N - MOVING, last)]
+        old_parts = [keep.tile([P, cols.stop - cols.start], F32, name="old%d" % i) for i, (first, cols) in enumerate(parts)]
+
+        nc.sync.dma_start(out=x_words[0][:].bitcast(I32), in_=xt_words[0].bitcast(I32))
+        nc.sync.dma_start(offsets[:], offs)
+        nc.sync.dma_start(out=x_rows[0:32, :].bitcast(I32), in_=xt_scales.rearrange("z q c -> (z q) c").bitcast(I32))
+        nc.sync.dma_start(out=x_words[1][:].bitcast(I32), in_=xt_words[1].bitcast(I32))
+        nc.sync.dma_start(out=low_codes[:].bitcast(I32), in_=low_words.rearrange("z p n t -> p z (n t)").bitcast(I32))
+        nc.sync.dma_start(out=weights[:], in_=cj.rearrange("o (p t) -> (o p) t", t=PACK))
+        nc.sync.dma_start(out=old_parts[2][:], in_=old[:, last])
+        for i in range(G_TILES):
+            nc.sync.dma_start(out=g_rows[i][:], in_=g[i * P : (i + 1) * P, :])
+        for i in range(2):
+            nc.sync.dma_start(out=old_parts[i][:], in_=old[:, parts[i][1]])
+
+        nc.vector.memset(x_rows[32:64, :].bitcast(I32), 0)
+        nc.vector.memset(x_rows[64:128, :].bitcast(I32), 0)
+        nc.vector.memset(low_plane[:].bitcast(I32), 0)
+        nc.vector.memset(x_plane[:].bitcast(I32), 0)
+        make_identity(nc, ident[:])
+        for q in range(4):
+            nc.gpsimd.dma_start(
+                out=low_plane[32 * q : 32 * q + 4, :, :].bitcast(I32),
+                in_=low_scales[:, 4 * q : 4 * q + 4, :].rearrange("z r c -> r z c").bitcast(I32),
+            )
+
+        x_picked_rows = keep.tile([P, J], U8, name="x_picked_rows", align_bytes=64)
+        nc.vector.tensor_copy(x_picked_rows[:], x_rows[:].indirect(offsets[:]))
+        for z in range(PASSES):
+            for q in range(4):
+                row = 16 * z + 4 * q
+                nc.gpsimd.dma_start(
+                    out=x_plane[32 * q : 32 * q + 4, z, :].bitcast(I32),
+                    in_=x_picked_rows[row : row + 4, :].bitcast(I32),
+                )
+        x_picked = [keep.tile([P, J], U16, name="x_picked%d" % z, align_bytes=64) for z in range(PASSES)]
+        for z in range(PASSES):
+            nc.vector.tensor_copy(x_picked[z][:], x_words[z][:].indirect(offsets[:]))
+
+        old_half = keep.tile([P, P], F32, name="old_half")
+        nc.scalar.activation(out=old_half[:], in_=old_parts[2][:], func=COPY, scale=OLD_SHARE)
+
+        g_codes = keep.tile([P, N], U32, name="g_codes", align_bytes=64)
+        g_plane = keep.tile([P, N], U8, name="g_plane", align_bytes=64)
+
+        ut_codes = keep.tile([P, R], U32, name="ut_codes", align_bytes=64)
+        ut_plane = keep.tile([P, R], U8, name="ut_plane", align_bytes=64)
+        banks = [psum.tile([P, MOVING], F32, name="bank%d" % b) for b in range(3)]
+
+        def quantize_ut(u_acc):
+            for z in range(PASSES):
+                nc.tensor.matmul_mx(
+                    out=u_acc[:],
+                    lhsT=low_codes[:, z, :].bitcast(E4M3),
+                    lhsT_scale=low_plane[:, z, :],
+                    rhs=x_picked[z][:].bitcast(E2M1),
+                    rhs_scale=x_plane[:, z, :],
+                    start=(z == 0),
+                    stop=(z == PASSES - 1),
+                )
+            u_dealt = keep.tile([P, PACK, P], F32, name="u_dealt")
+            nc.scalar.copy(out=u_dealt[:], in_=u_acc[:].rearrange("r (p t) -> r t p", t=PACK))
+            u_turned = psum.tile([P, PACK, R], F32, name="u_turned")
+            for t in range(PACK):
+                nc.tensor.transpose(u_turned[:, t, :], u_dealt[:, t, :], ident[:])
+            ut_bf = keep.tile([P, R, PACK], BF16, name="ut_bf", align_bytes=64)
+            nc.vector.tensor_tensor(
+                out=ut_bf[:],
+                in0=u_turned[:].rearrange("p t r -> p r t"),
+                in1=weights[:].unsqueeze(1).to_broadcast([P, R, PACK]),
+                op=MULT,
+            )
+            nc.vector.quantize_mx(
+                out=ut_codes[:].bitcast(E4M3), scales=ut_plane[:], in_=ut_bf[:].rearrange("p r t -> p (r t)")
+            )
+
+        def quantize_g(i, bank):
+            picked = ring.tile([P, J], BF16, name="picked", align_bytes=64)
+            nc.vector.tensor_copy(picked[:], g_rows[i][:].indirect(offsets[:]))
+            pairs = picked[:].bitcast(F32)
+            turned = bank[:, 0 : 2 * P].rearrange("p (h n) -> p h n", h=2)
+            for h in range(2):
+                nc.tensor.transpose(turned[:, h, :], pairs[:, h : J // 2 : 2], ident[:])
+            woven = ring.tile([P, P * PACK], BF16, name="woven", align_bytes=64)
+            nc.scalar.copy(
+                out=woven[:].bitcast(F32).rearrange("p (n h) -> p n h", h=2),
+                in_=turned.rearrange("p h n -> p n h"),
+            )
+            cols = slice(i * P, (i + 1) * P)
+            nc.vector.quantize_mx(out=g_codes[:, cols].bitcast(E5M2), scales=g_plane[:, cols], in_=woven[:])
+
+        def product(i):
+            first, cols = parts[i]
+            window = slice(first, first + MOVING)
+            acc = psum.tile([P, MOVING], F32, name="w_acc%d" % i)
+            nc.tensor.matmul_mx(
+                out=acc[:],
+                lhsT=ut_codes[:].bitcast(E4M3),
+                lhsT_scale=ut_plane[:],
+                rhs=g_codes[:, window].bitcast(E5M2),
+                rhs_scale=g_plane[:, window],
+                start=True,
+                stop=True,
+            )
+            return acc[:, cols.start - first : cols.stop - first]
+
+        def finish(i, scaled_here, share, scaled_before):
+            cols = parts[i][1]
+            result = keep.tile([P, cols.stop - cols.start], F32, name="result%d" % i)
+            nc.vector.scalar_tensor_tensor(out=result[:], in0=scaled_here, scalar=share, in1=scaled_before, op0=MULT, op1=ADD)
+            nc.sync.dma_start(out=out[:, cols], in_=result[:])
+
+        w_scaled = []
+        for i in range(G_TILES - 1):
+            if i == U_AFTER:
+                quantize_g(i, banks[2])
+                quantize_ut(banks[2])
+            else:
+                quantize_g(i, banks[i % 2])
+            for n in range(2):
+                if (i + 1) * P == parts[n][1].stop:
+                    w = product(n)
+                    scaled = keep.tile([P, w.shape[1]], F32, name="w_scaled%d" % n)
+                    nc.scalar.activation(out=scaled[:], in_=w, func=COPY, scale=W_SHARE)
+                    w_scaled.append(scaled)
+        quantize_g(G_TILES - 1, banks[1])
+        w_last = product(2)
+        for n in range(2):
+            finish(n, old_parts[n][:], OLD_SHARE, w_scaled[n][:])
+        finish(2, w_last, W_SHARE, old_half[:])

@@ -26,7 +26,6 @@ G_TILES = N // P
 MOVING = 512
 W_SHARE = 0.04
 OLD_SHARE = 0.5
-U_AFTER = 3
 
 
 def tile_list_adapter_up_grad_kernel(tc, xt_words, xt_scales, low_words, low_scales, cj, g, old, offs, out):
@@ -35,68 +34,64 @@ def tile_list_adapter_up_grad_kernel(tc, xt_words, xt_scales, low_words, low_sca
         keep = ctx.enter_context(tc.tile_pool(name="keep", bufs=1))
         ring = ctx.enter_context(tc.tile_pool(name="ring", bufs=3))
         psum = ctx.enter_context(tc.psum_pool(name="psum", bufs=1))
+        turn = ctx.enter_context(tc.psum_pool(name="turn", bufs=3))
 
         offsets = keep.tile([P, J // 16], U16, name="offsets")
         x_words = [keep.tile([P, T], U16, name="x_words%d" % z, align_bytes=64) for z in range(PASSES)]
-        x_rows = keep.tile([P, T], U8, name="x_rows", align_bytes=64)
+        x_rows = keep.tile([P, PASSES, T], U8, name="x_rows", align_bytes=64)
         low_codes = keep.tile([P, PASSES, R], U32, name="low_codes", align_bytes=64)
         low_plane = keep.tile([P, PASSES, R], U8, name="low_plane", align_bytes=64)
         x_plane = keep.tile([P, PASSES, J], U8, name="x_plane", align_bytes=64)
         weights = keep.tile([P, PACK], F32, name="weights")
-        g_rows = [keep.tile([P, T], F32, name="g_rows%d" % i, align_bytes=64) for i in range(G_TILES)]
+        g_rows = [keep.tile([P, T], F32, name="g_rows%d" % i, tag="slot%d" % i, align_bytes=64) for i in range(G_TILES)]
         ident = keep.tile([P, P], F32, name="ident")
 
-        last = slice(N - P, N)
-        parts = [(0, slice(0, MOVING)), (N - P - MOVING, slice(MOVING, N - P)), (N - MOVING, last)]
-        old_parts = [keep.tile([P, cols.stop - cols.start], F32, name="old%d" % i) for i, (first, cols) in enumerate(parts)]
+        old_halves = [keep.tile([P, MOVING], F32, name="old%d" % h) for h in range(2)]
 
-        nc.sync.dma_start(out=x_words[0][:].bitcast(I32), in_=xt_words[0].bitcast(I32))
-        nc.sync.dma_start(offsets[:], offs)
-        nc.sync.dma_start(out=x_rows[0:32, :].bitcast(I32), in_=xt_scales.rearrange("z q c -> (z q) c").bitcast(I32))
-        nc.sync.dma_start(out=x_words[1][:].bitcast(I32), in_=xt_words[1].bitcast(I32))
-        nc.sync.dma_start(out=low_codes[:].bitcast(I32), in_=low_words.rearrange("z p n t -> p z (n t)").bitcast(I32))
-        nc.sync.dma_start(out=weights[:], in_=cj.rearrange("o (p t) -> (o p) t", t=PACK))
-        nc.sync.dma_start(out=old_parts[2][:], in_=old[:, last])
-        for i in range(G_TILES):
-            nc.sync.dma_start(out=g_rows[i][:], in_=g[i * P : (i + 1) * P, :])
-        for i in range(2):
-            nc.sync.dma_start(out=old_parts[i][:], in_=old[:, parts[i][1]])
-
-        nc.vector.memset(x_rows[32:64, :].bitcast(I32), 0)
-        nc.vector.memset(x_rows[64:128, :].bitcast(I32), 0)
-        nc.vector.memset(low_plane[:].bitcast(I32), 0)
-        nc.vector.memset(x_plane[:].bitcast(I32), 0)
+        nc.gpsimd.memset(x_rows[:, 0, :].bitcast(I32), 0)
+        nc.vector.memset(x_rows[:, 1, :].bitcast(I32), 0)
+        nc.vector.memset(low_plane[:].rearrange("p z c -> p (z c)").bitcast(I32), 0)
         make_identity(nc, ident[:])
-        for q in range(4):
-            nc.gpsimd.dma_start(
-                out=low_plane[32 * q : 32 * q + 4, :, :].bitcast(I32),
-                in_=low_scales[:, 4 * q : 4 * q + 4, :].rearrange("z r c -> r z c").bitcast(I32),
-            )
 
-        x_picked_rows = keep.tile([P, J], U8, name="x_picked_rows", align_bytes=64)
-        nc.vector.tensor_copy(x_picked_rows[:], x_rows[:].indirect(offsets[:]))
-        for z in range(PASSES):
+        def load_g(i):
+            nc.sync.dma_start(out=g_rows[i][:], in_=g[i * P : (i + 1) * P, :])
+
+        def load_x(z):
+            nc.sync.dma_start(out=x_words[z][:].bitcast(I32), in_=xt_words[z].bitcast(I32))
+
+        def load_scale_rows(plane, rows):
             for q in range(4):
-                row = 16 * z + 4 * q
-                nc.gpsimd.dma_start(
-                    out=x_plane[32 * q : 32 * q + 4, z, :].bitcast(I32),
-                    in_=x_picked_rows[row : row + 4, :].bitcast(I32),
+                nc.sync.dma_start(
+                    out=plane[32 * q : 32 * q + 4, :, :].bitcast(I32),
+                    in_=rows[:, 4 * q : 4 * q + 4, :].rearrange("z r c -> r z c").bitcast(I32),
                 )
+
+        nc.sync.dma_start(offsets[:], offs)
+        load_x(0)
+        load_x(1)
+        load_scale_rows(x_rows, xt_scales)
+        load_g(0)
+        load_g(1)
+        nc.sync.dma_start(out=low_codes[:].bitcast(I32), in_=low_words.rearrange("z p n t -> p z (n t)").bitcast(I32))
+        load_g(2)
+        load_scale_rows(low_plane, low_scales)
+        load_g(3)
+        nc.sync.dma_start(out=weights[:], in_=cj.rearrange("o (p t) -> (o p) t", t=PACK))
+        for i in range(4, G_TILES):
+            load_g(i)
+        for h in (1, 0):
+            nc.sync.dma_start(out=old_halves[h][:], in_=old[:, h * MOVING : (h + 1) * MOVING])
+
         x_picked = [keep.tile([P, J], U16, name="x_picked%d" % z, align_bytes=64) for z in range(PASSES)]
         for z in range(PASSES):
             nc.vector.tensor_copy(x_picked[z][:], x_words[z][:].indirect(offsets[:]))
-
-        old_half = keep.tile([P, P], F32, name="old_half")
-        nc.scalar.activation(out=old_half[:], in_=old_parts[2][:], func=COPY, scale=OLD_SHARE)
-
-        g_codes = keep.tile([P, N], U32, name="g_codes", align_bytes=64)
-        g_plane = keep.tile([P, N], U8, name="g_plane", align_bytes=64)
+            nc.vector.tensor_copy(x_plane[:, z, :], x_rows[:, z, :].indirect(offsets[:]))
 
         ut_codes = keep.tile([P, R], U32, name="ut_codes", align_bytes=64)
         ut_plane = keep.tile([P, R], U8, name="ut_plane", align_bytes=64)
-        banks = [psum.tile([P, MOVING], F32, name="bank%d" % b) for b in range(3)]
 
-        def quantize_ut(u_acc):
+        def quantize_ut():
+            u_acc = psum.tile([P, J], F32, name="u_acc")
             for z in range(PASSES):
                 nc.tensor.matmul_mx(
                     out=u_acc[:],
@@ -112,7 +107,7 @@ def tile_list_adapter_up_grad_kernel(tc, xt_words, xt_scales, low_words, low_sca
             u_turned = psum.tile([P, PACK, R], F32, name="u_turned")
             for t in range(PACK):
                 nc.tensor.transpose(u_turned[:, t, :], u_dealt[:, t, :], ident[:])
-            ut_bf = keep.tile([P, R, PACK], BF16, name="ut_bf", align_bytes=64)
+            ut_bf = keep.tile([P, R, PACK], BF16, name="ut_bf", tag="slot3", align_bytes=64)
             nc.vector.tensor_tensor(
                 out=ut_bf[:],
                 in0=u_turned[:].rearrange("p t r -> p r t"),
@@ -123,57 +118,64 @@ def tile_list_adapter_up_grad_kernel(tc, xt_words, xt_scales, low_words, low_sca
                 out=ut_codes[:].bitcast(E4M3), scales=ut_plane[:], in_=ut_bf[:].rearrange("p r t -> p (r t)")
             )
 
-        def quantize_g(i, bank):
+        woven = keep.tile([P, N * PACK], BF16, name="woven", align_bytes=64)
+
+        def turn_g(i):
             picked = ring.tile([P, J], BF16, name="picked", align_bytes=64)
             nc.vector.tensor_copy(picked[:], g_rows[i][:].indirect(offsets[:]))
             pairs = picked[:].bitcast(F32)
-            turned = bank[:, 0 : 2 * P].rearrange("p (h n) -> p h n", h=2)
+            turned = turn.tile([P, 2, P], F32, name="turned")
             for h in range(2):
                 nc.tensor.transpose(turned[:, h, :], pairs[:, h : J // 2 : 2], ident[:])
-            woven = ring.tile([P, P * PACK], BF16, name="woven", align_bytes=64)
             nc.scalar.copy(
-                out=woven[:].bitcast(F32).rearrange("p (n h) -> p n h", h=2),
-                in_=turned.rearrange("p h n -> p n h"),
+                out=woven[:, i * J : (i + 1) * J].bitcast(F32).rearrange("p (n h) -> p n h", h=2),
+                in_=turned[:].rearrange("p h n -> p n h"),
             )
-            cols = slice(i * P, (i + 1) * P)
-            nc.vector.quantize_mx(out=g_codes[:, cols].bitcast(E5M2), scales=g_plane[:, cols], in_=woven[:])
 
-        def product(i):
-            first, cols = parts[i]
-            window = slice(first, first + MOVING)
-            acc = psum.tile([P, MOVING], F32, name="w_acc%d" % i)
+        def quantize_g(codes, plane, at, first, stop):
+            cols = slice(at * P, (at + stop - first) * P)
+            nc.vector.quantize_mx(
+                out=codes[:, cols].bitcast(E5M2), scales=plane[:, cols], in_=woven[:, first * J : stop * J]
+            )
+
+        def product(name, codes, plane, at):
+            window = slice(at * P, at * P + MOVING)
+            acc = psum.tile([P, MOVING], F32, name=name)
             nc.tensor.matmul_mx(
                 out=acc[:],
                 lhsT=ut_codes[:].bitcast(E4M3),
                 lhsT_scale=ut_plane[:],
-                rhs=g_codes[:, window].bitcast(E5M2),
-                rhs_scale=g_plane[:, window],
+                rhs=codes[:, window].bitcast(E5M2),
+                rhs_scale=plane[:, window],
                 start=True,
                 stop=True,
             )
-            return acc[:, cols.start - first : cols.stop - first]
+            return acc
 
-        def finish(i, scaled_here, share, scaled_before):
-            cols = parts[i][1]
-            result = keep.tile([P, cols.stop - cols.start], F32, name="result%d" % i)
+        def finish(cols, scaled_here, share, scaled_before):
+            result = keep.tile([P, cols.stop - cols.start], F32, name="result%d" % cols.start)
             nc.vector.scalar_tensor_tensor(out=result[:], in0=scaled_here, scalar=share, in1=scaled_before, op0=MULT, op1=ADD)
             nc.sync.dma_start(out=out[:, cols], in_=result[:])
 
-        w_scaled = []
-        for i in range(G_TILES - 1):
-            if i == U_AFTER:
-                quantize_g(i, banks[2])
-                quantize_ut(banks[2])
-            else:
-                quantize_g(i, banks[i % 2])
-            for n in range(2):
-                if (i + 1) * P == parts[n][1].stop:
-                    w = product(n)
-                    scaled = keep.tile([P, w.shape[1]], F32, name="w_scaled%d" % n)
-                    nc.scalar.activation(out=scaled[:], in_=w, func=COPY, scale=W_SHARE)
-                    w_scaled.append(scaled)
-        quantize_g(G_TILES - 1, banks[1])
-        w_last = product(2)
-        for n in range(2):
-            finish(n, old_parts[n][:], OLD_SHARE, w_scaled[n][:])
-        finish(2, w_last, W_SHARE, old_half[:])
+        for i in range(0, 4):
+            turn_g(i)
+        quantize_ut()
+        turn_g(4)
+        early_codes = keep.tile([P, MOVING], U32, name="early_codes", tag="slot4", align_bytes=64)
+        early_plane = keep.tile([P, MOVING], U8, name="early_plane", align_bytes=64)
+        quantize_g(early_codes, early_plane, 0, 0, 4)
+        w_early = keep.tile([P, MOVING], F32, name="w_early")
+        nc.scalar.activation(out=w_early[:], in_=product("acc_early", early_codes, early_plane, 0)[:], func=COPY, scale=W_SHARE)
+        for i in range(5, G_TILES):
+            turn_g(i)
+        late_codes = keep.tile([P, MOVING + P], U32, name="late_codes", tag="slot7", align_bytes=64)
+        late_plane = keep.tile([P, MOVING + P], U8, name="late_plane", align_bytes=64)
+        quantize_g(late_codes, late_plane, 0, 3, 7)
+        old_scaled = keep.tile([P, MOVING], F32, name="old_scaled")
+        nc.scalar.activation(out=old_scaled[:], in_=old_halves[1][:], func=COPY, scale=OLD_SHARE)
+        acc_mid = product("acc_mid", late_codes, late_plane, 0)
+        finish(slice(0, MOVING), old_halves[0][:], OLD_SHARE, w_early[:])
+        quantize_g(late_codes, late_plane, 4, 7, 8)
+        acc_last = product("acc_last", late_codes, late_plane, 1)
+        finish(slice(MOVING, N - P), acc_mid[:, P:], W_SHARE, old_scaled[:, : MOVING - P])
+        finish(slice(N - P, N), acc_last[:, MOVING - P :], W_SHARE, old_scaled[:, MOVING - P :])

@@ -40,8 +40,7 @@ def tile_list_adapter_up_grad_kernel(tc, xt_words, xt_scales, low_words, low_sca
         x_words = [keep.tile([P, T], U16, name="x_words%d" % z, align_bytes=64) for z in range(PASSES)]
         x_rows = keep.tile([P, PASSES, T], U8, name="x_rows", align_bytes=64)
         low_codes = keep.tile([P, PASSES, R], U32, name="low_codes", align_bytes=64)
-        low_plane = keep.tile([P, PASSES, R], U8, name="low_plane", align_bytes=64)
-        x_plane = keep.tile([P, PASSES, J], U8, name="x_plane", align_bytes=64)
+        planes = keep.tile([P, PASSES, J + R], U8, name="planes", align_bytes=64)
         weights = keep.tile([P, PACK], F32, name="weights")
         g_rows = [keep.tile([P, T], F32, name="g_rows%d" % i, tag="slot%d" % i, align_bytes=64) for i in range(G_TILES)]
         ident = keep.tile([P, P], F32, name="ident")
@@ -50,7 +49,7 @@ def tile_list_adapter_up_grad_kernel(tc, xt_words, xt_scales, low_words, low_sca
 
         nc.gpsimd.memset(x_rows[:, 0, :].bitcast(I32), 0)
         nc.vector.memset(x_rows[:, 1, :].bitcast(I32), 0)
-        nc.vector.memset(low_plane[:].rearrange("p z c -> p (z c)").bitcast(I32), 0)
+        nc.vector.memset(planes[:, :, J:].bitcast(I32), 0)
         make_identity(nc, ident[:])
 
         def load_g(i):
@@ -59,33 +58,29 @@ def tile_list_adapter_up_grad_kernel(tc, xt_words, xt_scales, low_words, low_sca
         def load_x(z):
             nc.sync.dma_start(out=x_words[z][:].bitcast(I32), in_=xt_words[z].bitcast(I32))
 
-        def load_scale_rows(plane, rows):
-            for q in range(4):
-                nc.sync.dma_start(
-                    out=plane[32 * q : 32 * q + 4, :, :].bitcast(I32),
-                    in_=rows[:, 4 * q : 4 * q + 4, :].rearrange("z r c -> r z c").bitcast(I32),
-                )
+        x_picked_rows = keep.tile([P, PASSES, J], U8, name="x_picked_rows", align_bytes=64)
+        x_picked = [keep.tile([P, J], U16, name="x_picked%d" % z, align_bytes=64) for z in range(PASSES)]
 
-        nc.sync.dma_start(offsets[:], offs)
-        load_x(0)
-        load_x(1)
-        load_scale_rows(x_rows, xt_scales)
         load_g(0)
+        nc.sync.dma_start(offsets[:], offs)
+        nc.sync.dma_start(out=x_rows[0:P:8, :, :].bitcast(I32), in_=xt_scales.rearrange("z q c -> q z c").bitcast(I32))
         load_g(1)
+        nc.sync.dma_start(out=planes[0:P:8, :, J:].bitcast(I32), in_=low_scales.rearrange("z q c -> q z c").bitcast(I32))
+        load_x(0)
         nc.sync.dma_start(out=low_codes[:].bitcast(I32), in_=low_words.rearrange("z p n t -> p z (n t)").bitcast(I32))
+        load_x(1)
         load_g(2)
-        load_scale_rows(low_plane, low_scales)
-        load_g(3)
         nc.sync.dma_start(out=weights[:], in_=cj.rearrange("o (p t) -> (o p) t", t=PACK))
+        for z in range(PASSES):
+            nc.vector.tensor_copy(x_picked_rows[:, z, :], x_rows[:, z, :].indirect(offsets[:]))
+        nc.vector.tensor_copy(planes[:, :, :J].bitcast(I32), x_picked_rows[:].bitcast(I32))
+        for r in range(1, 4):
+            nc.sync.dma_start(out=planes[r:P:32, :, :].bitcast(I32), in_=planes[8 * r : P : 32, :, :].bitcast(I32))
+        load_g(3)
         for i in range(4, G_TILES):
             load_g(i)
         for h in (1, 0):
             nc.sync.dma_start(out=old_halves[h][:], in_=old[:, h * MOVING : (h + 1) * MOVING])
-
-        x_picked = [keep.tile([P, J], U16, name="x_picked%d" % z, align_bytes=64) for z in range(PASSES)]
-        for z in range(PASSES):
-            nc.vector.tensor_copy(x_picked[z][:], x_words[z][:].indirect(offsets[:]))
-            nc.vector.tensor_copy(x_plane[:, z, :], x_rows[:, z, :].indirect(offsets[:]))
 
         ut_codes = keep.tile([P, R], U32, name="ut_codes", align_bytes=64)
         ut_plane = keep.tile([P, R], U8, name="ut_plane", align_bytes=64)
@@ -96,9 +91,9 @@ def tile_list_adapter_up_grad_kernel(tc, xt_words, xt_scales, low_words, low_sca
                 nc.tensor.matmul_mx(
                     out=u_acc[:],
                     lhsT=low_codes[:, z, :].bitcast(E4M3),
-                    lhsT_scale=low_plane[:, z, :],
+                    lhsT_scale=planes[:, z, J:],
                     rhs=x_picked[z][:].bitcast(E2M1),
-                    rhs_scale=x_plane[:, z, :],
+                    rhs_scale=planes[:, z, :J],
                     start=(z == 0),
                     stop=(z == PASSES - 1),
                 )
@@ -157,8 +152,12 @@ def tile_list_adapter_up_grad_kernel(tc, xt_words, xt_scales, low_words, low_sca
             nc.vector.scalar_tensor_tensor(out=result[:], in0=scaled_here, scalar=share, in1=scaled_before, op0=MULT, op1=ADD)
             nc.sync.dma_start(out=out[:, cols], in_=result[:])
 
-        for i in range(0, 4):
-            turn_g(i)
+        turn_g(0)
+        turn_g(1)
+        for z in range(PASSES):
+            nc.vector.tensor_copy(x_picked[z][:], x_words[z][:].indirect(offsets[:]))
+        turn_g(2)
+        turn_g(3)
         quantize_ut()
         turn_g(4)
         early_codes = keep.tile([P, MOVING], U32, name="early_codes", tag="slot4", align_bytes=64)

from contextlib import ExitStack

import concourse.mybir as mybir
from concourse.masks import make_identity

K, R, N, T, J = 1024, 128, 1024, 2048, 512
FLOPS = 2 * K * R * J + 2 * J * R * N

F32 = mybir.dt.float32
BF16 = mybir.dt.bfloat16
I32 = mybir.dt.int32
U32 = mybir.dt.uint32
U16 = mybir.dt.uint16
U8 = mybir.dt.uint8
E4M3 = mybir.dt.float8_e4m3fn_x4
E5M2 = mybir.dt.float8_e5m2_x4
E2M1 = mybir.dt.float4_e2m1fn_x4
MULT = mybir.AluOpType.mult
ADD = mybir.AluOpType.add
COPY = mybir.ActivationFunctionType.Copy

P = 128
PACK = 4
PASSES = K // (P * PACK)
G_TILES = N // P
MOVING = 512
W_SHARE = 0.04
OLD_SHARE = 0.5


def tile_list_adapter_up_grad_kernel(tc, xt_words, xt_scales, low_words, low_scales, cj, g, old, offs, out):
    nc = tc.nc
    with ExitStack() as ctx:
        keep = ctx.enter_context(tc.tile_pool(name="keep", bufs=1))
        ring = ctx.enter_context(tc.tile_pool(name="ring", bufs=3))
        psum = ctx.enter_context(tc.psum_pool(name="psum", bufs=1))
        turn = ctx.enter_context(tc.psum_pool(name="turn", bufs=3))

        offsets = keep.tile([P, J // 16], U16, name="offsets")
        x_words = [keep.tile([P, T], U16, name="x_words%d" % z, align_bytes=64) for z in range(PASSES)]
        x_rows = keep.tile([P, PASSES, T], U8, name="x_rows", align_bytes=64)
        low_codes = keep.tile([P, PASSES, R], U32, name="low_codes", align_bytes=64)
        planes = keep.tile([P, PASSES, J + R], U8, name="planes", align_bytes=64)
        weights = keep.tile([P, PACK], F32, name="weights")
        g_rows = [keep.tile([P, T], F32, name="g_rows%d" % i, tag="slot%d" % i, align_bytes=64) for i in range(G_TILES)]
        ident = keep.tile([P, P], F32, name="ident")

        old_halves = [keep.tile([P, MOVING], F32, name="old%d" % h) for h in range(2)]

        nc.gpsimd.memset(x_rows[:, 0, :].bitcast(I32), 0)
        nc.vector.memset(x_rows[:, 1, :].bitcast(I32), 0)
        nc.vector.memset(planes[:, :, J:].bitcast(I32), 0)
        make_identity(nc, ident[:])

        def load_g(i):
            nc.sync.dma_start(out=g_rows[i][:], in_=g[i * P : (i + 1) * P, :])

        def load_x(z):
            nc.sync.dma_start(out=x_words[z][:].bitcast(I32), in_=xt_words[z].bitcast(I32))

        x_picked_rows = keep.tile([P, PASSES, J], U8, name="x_picked_rows", align_bytes=64)
        x_picked = [keep.tile([P, J], U16, name="x_picked%d" % z, align_bytes=64) for z in range(PASSES)]

        load_g(0)
        nc.sync.dma_start(offsets[:], offs)
        nc.sync.dma_start(out=x_rows[0:P:8, :, :].bitcast(I32), in_=xt_scales.rearrange("z q c -> q z c").bitcast(I32))
        load_g(1)
        nc.sync.dma_start(out=planes[0:P:8, :, J:].bitcast(I32), in_=low_scales.rearrange("z q c -> q z c").bitcast(I32))
        load_x(0)
        nc.sync.dma_start(out=low_codes[:].bitcast(I32), in_=low_words.rearrange("z p n t -> p z (n t)").bitcast(I32))
        load_x(1)
        load_g(2)
        nc.sync.dma_start(out=weights[:], in_=cj.rearrange("o (p t) -> (o p) t", t=PACK))
        for z in range(PASSES):
            nc.vector.tensor_copy(x_picked_rows[:, z, :], x_rows[:, z, :].indirect(offsets[:]))
        nc.vector.tensor_copy(planes[:, :, :J].bitcast(I32), x_picked_rows[:].bitcast(I32))
        for r in range(1, 4):
            nc.sync.dma_start(out=planes[r:P:32, :, :].bitcast(I32), in_=planes[8 * r : P : 32, :, :].bitcast(I32))
        load_g(3)
        for i in range(4, G_TILES):
            load_g(i)
        for h in (1, 0):
            nc.sync.dma_start(out=old_halves[h][:], in_=old[:, h * MOVING : (h + 1) * MOVING])

        ut_codes = keep.tile([P, R], U32, name="ut_codes", align_bytes=64)
        ut_plane = keep.tile([P, R], U8, name="ut_plane", align_bytes=64)

        def quantize_ut():
            u_acc = psum.tile([P, J], F32, name="u_acc")
            for z in range(PASSES):
                nc.tensor.matmul_mx(
                    out=u_acc[:],
                    lhsT=low_codes[:, z, :].bitcast(E4M3),
                    lhsT_scale=planes[:, z, J:],
                    rhs=x_picked[z][:].bitcast(E2M1),
                    rhs_scale=planes[:, z, :J],
                    start=(z == 0),
                    stop=(z == PASSES - 1),
                )
            u_dealt = keep.tile([P, PACK, P], F32, name="u_dealt")
            nc.scalar.copy(out=u_dealt[:], in_=u_acc[:].rearrange("r (p t) -> r t p", t=PACK))
            u_turned = psum.tile([P, PACK, R], F32, name="u_turned")
            for t in range(PACK):
                nc.tensor.transpose(u_turned[:, t, :], u_dealt[:, t, :], ident[:])
            ut_bf = keep.tile([P, R, PACK], BF16, name="ut_bf", tag="slot3", align_bytes=64)
            nc.vector.tensor_tensor(
                out=ut_bf[:],
                in0=u_turned[:].rearrange("p t r -> p r t"),
                in1=weights[:].unsqueeze(1).to_broadcast([P, R, PACK]),
                op=MULT,
            )
            nc.vector.quantize_mx(
                out=ut_codes[:].bitcast(E4M3), scales=ut_plane[:], in_=ut_bf[:].rearrange("p r t -> p (r t)")
            )

        woven = keep.tile([P, N * PACK], BF16, name="woven", align_bytes=64)

        def turn_g(i):
            picked = ring.tile([P, J], BF16, name="picked", align_bytes=64)
            nc.vector.tensor_copy(picked[:], g_rows[i][:].indirect(offsets[:]))
            pairs = picked[:].bitcast(F32)
            turned = turn.tile([P, 2, P], F32, name="turned")
            for h in range(2):
                nc.tensor.transpose(turned[:, h, :], pairs[:, h : J // 2 : 2], ident[:])
            nc.scalar.copy(
                out=woven[:, i * J : (i + 1) * J].bitcast(F32).rearrange("p (n h) -> p n h", h=2),
                in_=turned[:].rearrange("p h n -> p n h"),
            )

        def quantize_g(codes, plane, at, first, stop):
            cols = slice(at * P, (at + stop - first) * P)
            nc.vector.quantize_mx(
                out=codes[:, cols].bitcast(E5M2), scales=plane[:, cols], in_=woven[:, first * J : stop * J]
            )

        def product(name, codes, plane, at):
            window = slice(at * P, at * P + MOVING)
            acc = psum.tile([P, MOVING], F32, name=name)
            nc.tensor.matmul_mx(
                out=acc[:],
                lhsT=ut_codes[:].bitcast(E4M3),
                lhsT_scale=ut_plane[:],
                rhs=codes[:, window].bitcast(E5M2),
                rhs_scale=plane[:, window],
                start=True,
                stop=True,
            )
            return acc

        def finish(cols, scaled_here, share, scaled_before):
            result = keep.tile([P, cols.stop - cols.start], F32, name="result%d" % cols.start)
            nc.vector.scalar_tensor_tensor(out=result[:], in0=scaled_here, scalar=share, in1=scaled_before, op0=MULT, op1=ADD)
            nc.sync.dma_start(out=out[:, cols], in_=result[:])

        turn_g(0)
        turn_g(1)
        for z in range(PASSES):
            nc.vector.tensor_copy(x_picked[z][:], x_words[z][:].indirect(offsets[:]))
        turn_g(2)
        turn_g(3)
        quantize_ut()
        turn_g(4)
        early_codes = keep.tile([P, MOVING], U32, name="early_codes", tag="slot4", align_bytes=64)
        early_plane = keep.tile([P, MOVING], U8, name="early_plane", align_bytes=64)
        quantize_g(early_codes, early_plane, 0, 0, 4)
        w_early = keep.tile([P, MOVING], F32, name="w_early")
        nc.scalar.activation(out=w_early[:], in_=product("acc_early", early_codes, early_plane, 0)[:], func=COPY, scale=W_SHARE)
        for i in range(5, G_TILES):
            turn_g(i)
        late_codes = keep.tile([P, MOVING + P], U32, name="late_codes", tag="slot7", align_bytes=64)
        late_plane = keep.tile([P, MOVING + P], U8, name="late_plane", align_bytes=64)
        quantize_g(late_codes, late_plane, 0, 3, 7)
        old_scaled = keep.tile([P, MOVING], F32, name="old_scaled")
        nc.scalar.activation(out=old_scaled[:], in_=old_halves[1][:], func=COPY, scale=OLD_SHARE)
        acc_mid = product("acc_mid", late_codes, late_plane, 0)
        finish(slice(0, MOVING), old_halves[0][:], OLD_SHARE, w_early[:])
        quantize_g(late_codes, late_plane, 4, 7, 8)
        acc_last = product("acc_last", late_codes, late_plane, 1)
        finish(slice(MOVING, N - P), acc_mid[:, P:], W_SHARE, old_scaled[:, : MOVING - P])
        finish(slice(N - P, N), acc_last[:, MOVING - P :], W_SHARE, old_scaled[:, MOVING - P :])
